import numpy as np
import ml_dtypes


def mxq(x, axis, fmt="e4m3"):
    dtype, down = {"e4m3": (ml_dtypes.float8_e4m3fn, 7), "e5m2": (ml_dtypes.float8_e5m2, 14)}[fmt]
    v = np.moveaxis(np.asarray(x, np.float32).astype(ml_dtypes.bfloat16).astype(np.float64), axis, -1)
    blocks = v.reshape(v.shape[:-1] + (-1, 32))
    amax = np.abs(blocks).max(-1, keepdims=True)
    byte = np.maximum(np.where(amax > 0, np.frexp(amax)[1] - 1 + 127, 0) - down, 1)
    scale = np.exp2(byte - 127.0)
    codes = (blocks / scale).astype(np.float32).astype(dtype).astype(np.float64)
    return np.moveaxis((codes * scale).reshape(v.shape), -1, axis)


WIDE = False


def mx_kscale(k):
    if not WIDE:
        return np.ones(k)
    levels = np.array([10, -10, 5, -5, 0])
    if k % 512:
        return np.exp2(np.random.permutation(np.resize(levels, k // 32))).repeat(32)
    a = np.empty((k // 512, 16))
    for p in range(k // 512):
        a[p, :8] = np.random.permutation(np.resize(levels, 8))
        for g in range(8):
            far = levels[np.abs(levels - a[p, g]) >= 10]
            a[p, g + 8] = far[np.random.randint(len(far))]
    return np.exp2(a.ravel()).repeat(32)


def f64(x):
    return np.asarray(x).astype(np.float64)


def striped(idx):
    return np.tile(np.asarray(idx).reshape(-1, 16).T, (8, 1)).astype(np.uint16)


def unstriped(offs):
    return offs[:16].T.reshape(-1).astype(np.int64)


E2M1 = np.array([0.0, 0.5, 1.0, 1.5, 2.0, 3.0, 4.0, 6.0, -0.0, -0.5, -1.0, -1.5, -2.0, -3.0, -4.0, -6.0])


def pack_weight(w, fmt):
    k, n = w.shape
    w = f64(np.asarray(w, np.float32).astype(ml_dtypes.bfloat16)).reshape(k // 32, 32, n)
    amax = np.abs(w).max(1)
    if fmt == "e4m3":
        byte = np.frexp(amax)[1] - 1 + 127 - 7
    else:
        mant, ex = np.frexp(amax / 6.0)
        byte = np.where(mant > 0.5, ex, ex - 1) + 127
    byte = np.clip(np.where(amax > 0, byte, 1), 1, 254)
    scaled = (w * np.exp2(127.0 - byte)[:, None, :]).reshape(k, n).astype(np.float32)
    by_word = np.ascontiguousarray(scaled.reshape(k // 512, 128, 4, n).transpose(0, 1, 3, 2))
    if fmt == "e4m3":
        words = by_word.astype(ml_dtypes.float8_e4m3fn).view(np.uint8)
    else:
        c = by_word.astype(ml_dtypes.float4_e2m1fn).view(np.uint8) & 0xF
        words = (c[..., 0::2] | (c[..., 1::2] << 4)).reshape(k // 512, 128, 2 * n)
    return np.ascontiguousarray(words), np.ascontiguousarray(byte.astype(np.uint8).reshape(k // 512, 16, n))


def unpack_weight(words, scales, fmt):
    g, _, n = scales.shape
    words = np.ascontiguousarray(words).reshape(g, 128, n, -1)
    if fmt == "e4m3":
        vals = words.view(ml_dtypes.float8_e4m3fn).astype(np.float64)
    else:
        nib = np.empty((g, 128, n, 4), np.uint8)
        nib[..., 0::2] = words & 0xF
        nib[..., 1::2] = words >> 4
        vals = E2M1[nib]
    vals = vals * np.repeat(np.exp2(scales.astype(np.float64) - 127.0), 8, axis=1)[..., None]
    return vals.transpose(0, 1, 3, 2).reshape(g * 512, n)


C, I, T, L, N = 2048, 512, 512, 512, 512


def setup_inputs():
    n = np.random.standard_normal
    idx = np.random.permutation(C)[:I]
    idx2 = np.random.permutation(C)[:I]
    fi = mx_kscale(I)
    fl = mx_kscale(L)
    wp = pack_weight(n((I, N)) * 1 / np.sqrt(I) * fi[:, None], "e2m1")
    cxp = pack_weight(n((L, T)) / fl[:, None], "e4m3")
    wcp = pack_weight(n((L, N)) * 1 / np.sqrt(L) * fl[:, None], "e2m1")
    return {
        "xt": (n((T, C))).astype(np.float32),
        "pf": (np.random.uniform(0.5, 2.0, (I, 1)) / fi[:, None]).astype(np.float32),
        "w_words": wp[0],
        "w_scales": wp[1],
        "cx_words": cxp[0],
        "cx_scales": cxp[1],
        "wc_words": wcp[0],
        "wc_scales": wcp[1],
        "offs": striped(idx),
        "offs2": striped(idx2),
    }


def reference(xt, pf, w_words, w_scales, cx_words, cx_scales, wc_words, wc_scales, offs, offs2):
    idx = unstriped(offs)
    idx2 = unstriped(offs2)
    wu = unpack_weight(w_words, w_scales, "e2m1")
    cxu = unpack_weight(cx_words, cx_scales, "e4m3")
    wcu = unpack_weight(wc_words, wc_scales, "e2m1")
    pr = f64(xt)[:, idx] * f64(xt)[:, idx2]
    pt = pr.T
    pw = pt * f64(pf)
    pwq = mxq(pw, 0, "e4m3")
    y = wu.T @ pwq + wcu.T @ cxu
    return y

@@ -1,0 +1,193 @@
+from contextlib import ExitStack
+
+import concourse.mybir as mybir
+from concourse.masks import make_identity
+
+C, I, T, L, N = 2048, 512, 512, 512, 512
+FLOPS = 2 * (I + L) * N * T
+
+F32 = mybir.dt.float32
+BF16 = mybir.dt.bfloat16
+I32 = mybir.dt.int32
+U32 = mybir.dt.uint32
+U16 = mybir.dt.uint16
+U8 = mybir.dt.uint8
+FP8X4 = mybir.dt.float8_e4m3fn_x4
+FP4X4 = mybir.dt.float4_e2m1fn_x4
+MULT = mybir.AluOpType.mult
+
+P = 128
+PACK = 4
+TILES = T // P
+ROWS = N // P
+HALF = I // 2
+
+
+def tile_list_feature_pairs_by_lists_kernel(
+    tc, xt, pf, w_words, w_scales, cx_words, cx_scales, wc_words, wc_scales, offs, offs2, out
+):
+    nc = tc.nc
+    with ExitStack() as ctx:
+        keep = ctx.enter_context(tc.tile_pool(name="keep", bufs=1))
+        psum = ctx.enter_context(tc.psum_pool(name="psum", bufs=1))
+
+        first = keep.tile([P, I // 16], U16, name="first")
+        second = keep.tile([P, I // 16], U16, name="second")
+        pf_col = keep.tile([P, PACK], F32, name="pf_col")
+        wc_plane = keep.tile([P, N], U8, name="wc_plane", align_bytes=64)
+        cx_plane = keep.tile([P, T], U8, name="cx_plane", align_bytes=64)
+        w_plane = keep.tile([P, N], U8, name="w_plane", align_bytes=64)
+        ident = keep.tile([P, P], F32, name="ident")
+        xs = [keep.tile([P, C], F32, name=f"x{b}") for b in range(TILES)]
+        w_sb = keep.tile([P, 2 * N], U8, name="w_sb", align_bytes=64)
+        wc_sb = keep.tile([P, 2 * N], U8, name="wc_sb", align_bytes=64)
+        cx_sb = [keep.tile([P, T // 2], U32, name=f"cx_sb{h}", tag=f"pairs{h + 1}", align_bytes=64) for h in range(2)]
+        cx_rows = cx_words[0].rearrange("p t r -> p (t r)").bitcast(I32)
+
+        nc.gpsimd.memset(wc_plane[:].bitcast(I32), 0)
+        nc.gpsimd.memset(cx_plane[:].bitcast(I32), 0)
+        nc.gpsimd.memset(w_plane[:].bitcast(I32), 0)
+        make_identity(nc, ident[:])
+
+        def load_rows(queue, plane, rows, quads):
+            for q in quads:
+                queue.dma_start(plane[32 * q : 32 * q + 4, :].bitcast(I32), rows[0, 4 * q : 4 * q + 4, :].bitcast(I32))
+
+        nc.sync.dma_start(first[:], offs)
+        nc.scalar.dma_start(pf_col[:], pf.rearrange("(p j) o -> p (j o)", j=PACK))
+        nc.sync.dma_start(second[:], offs2)
+        nc.sync.dma_start(xs[0][:], xt[0:P, :])
+        load_rows(nc.sync, wc_plane, wc_scales, range(4))
+        nc.sync.dma_start(xs[1][:], xt[P : 2 * P, :])
+        load_rows(nc.sync, cx_plane, cx_scales, range(2))
+        nc.sync.dma_start(cx_sb[0][:].bitcast(I32), cx_rows[:, 0 : T // 2])
+        nc.sync.dma_start(wc_sb[:].bitcast(I32), wc_words[0].bitcast(I32))
+        load_rows(nc.sync, cx_plane, cx_scales, range(2, 4))
+        nc.sync.dma_start(xs[2][:], xt[2 * P : 3 * P, :])
+        nc.sync.dma_start(cx_sb[1][:].bitcast(I32), cx_rows[:, T // 2 : T])
+        load_rows(nc.sync, w_plane, w_scales, range(4))
+        nc.sync.dma_start(w_sb[:].bitcast(I32), w_words[0].bitcast(I32))
+        nc.sync.dma_start(xs[3][:], xt[3 * P : 4 * P, :])
+
+        pf_ps = psum.tile([P, PACK, P], F32, name="pf_ps", tag="turn0")
+        for j in range(PACK):
+            nc.tensor.transpose(pf_ps[:, j, :], pf_col[:, j : j + 1].to_broadcast([P, P]), ident[:])
+        pf_rows = [keep.tile([P, HALF], F32, name=f"pf_row{h}", tag=f"pf_row{h}", align_bytes=64) for h in range(2)]
+        for h in range(2):
+            nc.vector.tensor_copy(
+                pf_rows[h][:].rearrange("q (p j) -> q p j", j=PACK),
+                pf_ps[:, :, h * 64 : (h + 1) * 64].rearrange("q j p -> q p j"),
+            )
+
+        out_v = out.rearrange("(m p) t -> p m t", p=P)
+
+        def gather(b, between):
+            parts = [keep.tile([P, HALF], F32, name=f"part{b}_{h}", tag=f"part{b}_{h}", align_bytes=64) for h in range(2)]
+            pw = [
+                keep.tile(
+                    [P, HALF], F32, name=f"pw{b}_{h}", align_bytes=64,
+                    tag=f"part{b - 1}_0" if (b, h) == (TILES - 1, 0) else f"pw{b}_{h}",
+                )
+                for h in range(2)
+            ]
+            for h in range(2):
+                o = slice(h * HALF // 16, (h + 1) * HALF // 16)
+                nc.vector.tensor_tensor(parts[h][:], xs[b][:].indirect(first[:, o]), pf_rows[h][:], MULT)
+            for h in range(2):
+                o = slice(h * HALF // 16, (h + 1) * HALF // 16)
+                if h == 1 and between is not None:
+                    between()
+                nc.vector.tensor_tensor(pw[h][:], xs[b][:].indirect(second[:, o]), parts[h][:], MULT)
+            return pw
+
+        def turn(b, pw):
+            pairs = keep.tile([P, 2, P, 2], BF16, name=f"pairs{b}", tag=f"pairs{b}", align_bytes=64)
+            for h in range(2):
+                nc.scalar.copy(pairs[:, :, h * 64 : (h + 1) * 64, :], pw[h][:].rearrange("t (p u e) -> t u p e", u=2, e=2))
+            words = pairs[:].rearrange("t u p e -> t (u p e)").bitcast(F32)
+            turned = psum.tile([P, 2, P], F32, name=f"turned{b}", tag=f"turn{b}" if b < 2 else f"acc{b - 2}_0")
+            for u in range(2):
+                nc.tensor.transpose(turned[:, u, :], words[:, u * P : (u + 1) * P], ident[:])
+            grouped = keep.tile([P, P * PACK], BF16, name=f"grouped{b}", align_bytes=64)
+            nc.scalar.copy(
+                grouped[:].bitcast(F32).rearrange("p (t u) -> p t u", u=2), turned[:].rearrange("p u t -> p t u")
+            )
+            return grouped
+
+        def quantise(b, grouped):
+            codes = keep.tile([P, P], U32, name=f"codes{b}", tag="pf_row1" if b == TILES - 2 else f"part{b + 1}_0", align_bytes=64)
+            scales = keep.tile([P, P], U8, name=f"scales{b}", align_bytes=64)
+            nc.vector.quantize_mx(out=codes[:].bitcast(FP8X4), scales=scales[:], in_=grouped[:])
+            return codes, scales
+
+        def groups_of(b):
+            return [(0, 1), (2, 3)] if b == TILES - 1 else [(0, 1, 2, 3)]
+
+        def linear(b):
+            tok = slice(b * P, (b + 1) * P)
+            banks = [
+                psum.tile([P, len(ms), P], F32, name=f"acc{b}_{g}", tag=f"acc{b}_{g}") for g, ms in enumerate(groups_of(b))
+            ]
+            for bank, ms in zip(banks, groups_of(b)):
+                for k, m in enumerate(ms):
+                    nc.tensor.matmul_mx(
+                        out=bank[:, k, :],
+                        lhsT=wc_sb[:, 2 * P * m : 2 * P * (m + 1)].bitcast(FP4X4),
+                        lhsT_scale=wc_plane[:, P * m : P * (m + 1)],
+                        rhs=cx_sb[b // 2][:, (b % 2) * P : (b % 2 + 1) * P].bitcast(FP8X4),
+                        rhs_scale=cx_plane[:, tok],
+                        start=(k == 0),
+                        stop=False,
+                    )
+            return banks
+
+        def multiply(b, banks, codes, scales):
+            tok = slice(b * P, (b + 1) * P)
+            last = b == TILES - 1
+            for g, (bank, ms) in enumerate(zip(banks, groups_of(b))):
+                for k, m in enumerate(ms):
+                    nc.tensor.matmul_mx(
+                        out=bank[:, k, :],
+                        lhsT=w_sb[:, 2 * P * m : 2 * P * (m + 1)].bitcast(FP4X4),
+                        lhsT_scale=w_plane[:, P * m : P * (m + 1)],
+                        rhs=codes[:].bitcast(FP8X4),
+                        rhs_scale=scales[:],
+                        start=False,
+                        stop=(k == len(ms) - 1),
+                    )
+                res = keep.tile([P, len(ms), P], F32, name=f"res{b}_{g}")
+                if last and g == 0:
+                    nc.vector.tensor_copy(res[:], bank[:])
+                    nc.sync.dma_start(out_v[:, ms[0] : ms[-1] + 1, tok], res[:])
+                elif last:
+                    nc.scalar.copy(res[:], bank[:])
+                    nc.scalar.dma_start(out_v[:, ms[0] : ms[-1] + 1, tok], res[:])
+                elif b == TILES - 2:
+                    nc.vector.tensor_copy(res[:], bank[:])
+                    nc.sync.dma_start(out_v[:, ms[0] : ms[-1] + 1, tok], res[:])
+                else:
+                    nc.scalar.copy(res[:], bank[:])
+                    nc.sync.dma_start(out_v[:, ms[0] : ms[-1] + 1, tok], res[:])
+
+        pws = {}
+        grouped = {}
+        made = {}
+        sums = {}
+
+        def quantise_before_last():
+            made[TILES - 2] = quantise(TILES - 2, grouped[TILES - 2])
+
+        for step in range(TILES):
+            last = step == TILES - 1
+            if step >= 2:
+                multiply(step - 2, sums[step - 2], *made[step - 2])
+            pws[step] = gather(step, quantise_before_last if last else None)
+            if last:
+                multiply(step - 1, sums[step - 1], *made[step - 1])
+            grouped[step] = turn(step, pws[step])
+            if step < 2:
+                for b in (2 * step, 2 * step + 1):
+                    sums[b] = linear(b)
+            if step >= 1 and not last:
+                made[step - 1] = quantise(step - 1, grouped[step - 1])
+        multiply(TILES - 1, sums[TILES - 1], *quantise(TILES - 1, grouped[TILES - 1]))

@@ -55,8 +55,8 @@ def tile_list_feature_pairs_by_lists_kernel(
 
         nc.sync.dma_start(first[:], offs)
         nc.scalar.dma_start(pf_col[:], pf.rearrange("(p j) o -> p (j o)", j=PACK))
-        nc.sync.dma_start(second[:], offs2)
         nc.sync.dma_start(xs[0][:], xt[0:P, :])
+        nc.sync.dma_start(second[:], offs2)
         load_rows(nc.sync, wc_plane, wc_scales, range(4))
         nc.sync.dma_start(xs[1][:], xt[P : 2 * P, :])
         load_rows(nc.sync, cx_plane, cx_scales, range(2))
@@ -81,31 +81,36 @@ def tile_list_feature_pairs_by_lists_kernel(
 
         out_v = out.rearrange("(m p) t -> p m t", p=P)
 
+        def pieces_of(b):
+            return [(0, 256), (256, 512)]
+
         def gather(b, between):
             parts = [keep.tile([P, HALF], F32, name=f"part{b}_{h}", tag=f"part{b}_{h}", align_bytes=64) for h in range(2)]
-            pw = [
-                keep.tile(
-                    [P, HALF], F32, name=f"pw{b}_{h}", align_bytes=64,
-                    tag=f"part{b - 1}_0" if (b, h) == (TILES - 1, 0) else f"pw{b}_{h}",
-                )
-                for h in range(2)
-            ]
             for h in range(2):
                 o = slice(h * HALF // 16, (h + 1) * HALF // 16)
                 nc.vector.tensor_tensor(parts[h][:], xs[b][:].indirect(first[:, o]), pf_rows[h][:], MULT)
-            for h in range(2):
-                o = slice(h * HALF // 16, (h + 1) * HALF // 16)
-                if h == 1 and between is not None:
+            pw = []
+            for k, (lo, hi) in enumerate(pieces_of(b)):
+                if k == 1 and between is not None:
                     between()
-                nc.vector.tensor_tensor(pw[h][:], xs[b][:].indirect(second[:, o]), parts[h][:], MULT)
+                piece = keep.tile(
+                    [P, hi - lo], F32, name=f"pw{b}_{k}", align_bytes=64,
+                    tag=f"part{b - 1}_0" if (b, k) == (TILES - 1, 0) else f"pw{b}_{k}",
+                )
+                h = lo // HALF
+                nc.vector.tensor_tensor(
+                    piece[:], xs[b][:].indirect(second[:, lo // 16 : hi // 16]), parts[h][:, lo - h * HALF : hi - h * HALF], MULT
+                )
+                pw.append(piece)
             return pw
 
         def turn(b, pw):
             pairs = keep.tile([P, 2, P, 2], BF16, name=f"pairs{b}", tag=f"pairs{b}", align_bytes=64)
-            for h in range(2):
-                nc.scalar.copy(pairs[:, :, h * 64 : (h + 1) * 64, :], pw[h][:].rearrange("t (p u e) -> t u p e", u=2, e=2))
+            for piece, (lo, hi) in zip(pw, pieces_of(b)):
+                cast = nc.vector.tensor_copy if (b, hi) == (TILES - 1, I) else nc.scalar.copy
+                cast(pairs[:, :, lo // PACK : hi // PACK, :], piece[:].rearrange("t (p u e) -> t u p e", u=2, e=2))
             words = pairs[:].rearrange("t u p e -> t (u p e)").bitcast(F32)
-            turned = psum.tile([P, 2, P], F32, name=f"turned{b}", tag=f"turn{b}" if b < 2 else f"acc{b - 2}_0")
+            turned = psum.tile([P, 2, P], F32, name=f"turned{b}", tag="turn0" if b < 2 else f"acc{b - 2}_0")
             for u in range(2):
                 nc.tensor.transpose(turned[:, u, :], words[:, u * P : (u + 1) * P], ident[:])
             grouped = keep.tile([P, P * PACK], BF16, name=f"grouped{b}", align_bytes=64)
@@ -121,7 +126,7 @@ def tile_list_feature_pairs_by_lists_kernel(
             return codes, scales
 
         def groups_of(b):
-            return [(0, 1), (2, 3)] if b == TILES - 1 else [(0, 1, 2, 3)]
+            return [(0,), (1,), (2,), (3,)] if b == TILES - 1 else [(0, 1, 2, 3)]
 
         def linear(b):
             tok = slice(b * P, (b + 1) * P)
@@ -156,27 +161,20 @@ def tile_list_feature_pairs_by_lists_kernel(
                         stop=(k == len(ms) - 1),
                     )
                 res = keep.tile([P, len(ms), P], F32, name=f"res{b}_{g}")
-                if last and g == 0:
+                if (last and g % 2 == 1) or b == TILES - 2:
                     nc.vector.tensor_copy(res[:], bank[:])
-                    nc.sync.dma_start(out_v[:, ms[0] : ms[-1] + 1, tok], res[:])
-                elif last:
-                    nc.scalar.copy(res[:], bank[:])
-                    nc.scalar.dma_start(out_v[:, ms[0] : ms[-1] + 1, tok], res[:])
-                elif b == TILES - 2:
-                    nc.vector.tensor_copy(res[:], bank[:])
-                    nc.sync.dma_start(out_v[:, ms[0] : ms[-1] + 1, tok], res[:])
                 else:
                     nc.scalar.copy(res[:], bank[:])
-                    nc.sync.dma_start(out_v[:, ms[0] : ms[-1] + 1, tok], res[:])
+                nc.sync.dma_start(out_v[:, ms[0] : ms[-1] + 1, tok], res[:])
 
         pws = {}
         grouped = {}
         made = {}
-        sums = {}
 
         def quantise_before_last():
             made[TILES - 2] = quantise(TILES - 2, grouped[TILES - 2])
 
+        sums = {}
         for step in range(TILES):
             last = step == TILES - 1
             if step >= 2:

@@ -41,7 +41,7 @@ def tile_list_feature_pairs_by_lists_kernel(
         xs = [keep.tile([P, C], F32, name=f"x{b}") for b in range(TILES)]
         w_sb = keep.tile([P, 2 * N], U8, name="w_sb", align_bytes=64)
         wc_sb = keep.tile([P, 2 * N], U8, name="wc_sb", align_bytes=64)
-        cx_sb = [keep.tile([P, T // 2], U32, name=f"cx_sb{h}", tag=f"pairs{h + 1}", align_bytes=64) for h in range(2)]
+        cx_sb = [keep.tile([P, T // 2], U32, name=f"cx_sb{h}", tag=("pairs1", "cx_late")[h], align_bytes=64) for h in range(2)]
         cx_rows = cx_words[0].rearrange("p t r -> p (t r)").bitcast(I32)
 
         nc.gpsimd.memset(wc_plane[:].bitcast(I32), 0)
@@ -64,10 +64,10 @@ def tile_list_feature_pairs_by_lists_kernel(
         nc.sync.dma_start(wc_sb[:].bitcast(I32), wc_words[0].bitcast(I32))
         load_rows(nc.sync, cx_plane, cx_scales, range(2, 4))
         nc.sync.dma_start(xs[2][:], xt[2 * P : 3 * P, :])
-        nc.sync.dma_start(cx_sb[1][:].bitcast(I32), cx_rows[:, T // 2 : T])
         load_rows(nc.sync, w_plane, w_scales, range(4))
         nc.sync.dma_start(w_sb[:].bitcast(I32), w_words[0].bitcast(I32))
         nc.sync.dma_start(xs[3][:], xt[3 * P : 4 * P, :])
+        nc.sync.dma_start(cx_sb[1][:].bitcast(I32), cx_rows[:, T // 2 : T])
 
         pf_ps = psum.tile([P, PACK, P], F32, name="pf_ps", tag="turn0")
         for j in range(PACK):

from contextlib import ExitStack

import concourse.mybir as mybir
from concourse.masks import make_identity

C, I, T, L, N = 2048, 512, 512, 512, 512
FLOPS = 2 * (I + L) * N * T

F32 = mybir.dt.float32
BF16 = mybir.dt.bfloat16
I32 = mybir.dt.int32
U32 = mybir.dt.uint32
U16 = mybir.dt.uint16
U8 = mybir.dt.uint8
FP8X4 = mybir.dt.float8_e4m3fn_x4
FP4X4 = mybir.dt.float4_e2m1fn_x4
MULT = mybir.AluOpType.mult

P = 128
PACK = 4
TILES = T // P
ROWS = N // P
HALF = I // 2


def tile_list_feature_pairs_by_lists_kernel(
    tc, xt, pf, w_words, w_scales, cx_words, cx_scales, wc_words, wc_scales, offs, offs2, out
):
    nc = tc.nc
    with ExitStack() as ctx:
        keep = ctx.enter_context(tc.tile_pool(name="keep", bufs=1))
        psum = ctx.enter_context(tc.psum_pool(name="psum", bufs=1))

        first = keep.tile([P, I // 16], U16, name="first")
        second = keep.tile([P, I // 16], U16, name="second")
        pf_col = keep.tile([P, PACK], F32, name="pf_col")
        wc_plane = keep.tile([P, N], U8, name="wc_plane", align_bytes=64)
        cx_plane = keep.tile([P, T], U8, name="cx_plane", align_bytes=64)
        w_plane = keep.tile([P, N], U8, name="w_plane", align_bytes=64)
        ident = keep.tile([P, P], F32, name="ident")
        xs = [keep.tile([P, C], F32, name=f"x{b}") for b in range(TILES)]
        w_sb = keep.tile([P, 2 * N], U8, name="w_sb", align_bytes=64)
        wc_sb = keep.tile([P, 2 * N], U8, name="wc_sb", align_bytes=64)
        cx_sb = [keep.tile([P, T // 2], U32, name=f"cx_sb{h}", tag=("pairs1", "cx_late")[h], align_bytes=64) for h in range(2)]
        cx_rows = cx_words[0].rearrange("p t r -> p (t r)").bitcast(I32)

        nc.gpsimd.memset(wc_plane[:].bitcast(I32), 0)
        nc.gpsimd.memset(cx_plane[:].bitcast(I32), 0)
        nc.gpsimd.memset(w_plane[:].bitcast(I32), 0)
        make_identity(nc, ident[:])

        def load_rows(queue, plane, rows, quads):
            for q in quads:
                queue.dma_start(plane[32 * q : 32 * q + 4, :].bitcast(I32), rows[0, 4 * q : 4 * q + 4, :].bitcast(I32))

        nc.sync.dma_start(first[:], offs)
        nc.scalar.dma_start(pf_col[:], pf.rearrange("(p j) o -> p (j o)", j=PACK))
        nc.sync.dma_start(xs[0][:], xt[0:P, :])
        nc.sync.dma_start(second[:], offs2)
        load_rows(nc.sync, wc_plane, wc_scales, range(4))
        nc.sync.dma_start(xs[1][:], xt[P : 2 * P, :])
        load_rows(nc.sync, cx_plane, cx_scales, range(2))
        nc.sync.dma_start(cx_sb[0][:].bitcast(I32), cx_rows[:, 0 : T // 2])
        nc.sync.dma_start(wc_sb[:].bitcast(I32), wc_words[0].bitcast(I32))
        load_rows(nc.sync, cx_plane, cx_scales, range(2, 4))
        nc.sync.dma_start(xs[2][:], xt[2 * P : 3 * P, :])
        load_rows(nc.sync, w_plane, w_scales, range(4))
        nc.sync.dma_start(w_sb[:].bitcast(I32), w_words[0].bitcast(I32))
        nc.sync.dma_start(xs[3][:], xt[3 * P : 4 * P, :])
        nc.sync.dma_start(cx_sb[1][:].bitcast(I32), cx_rows[:, T // 2 : T])

        pf_ps = psum.tile([P, PACK, P], F32, name="pf_ps", tag="turn0")
        for j in range(PACK):
            nc.tensor.transpose(pf_ps[:, j, :], pf_col[:, j : j + 1].to_broadcast([P, P]), ident[:])
        pf_rows = [keep.tile([P, HALF], F32, name=f"pf_row{h}", tag=f"pf_row{h}", align_bytes=64) for h in range(2)]
        for h in range(2):
            nc.vector.tensor_copy(
                pf_rows[h][:].rearrange("q (p j) -> q p j", j=PACK),
                pf_ps[:, :, h * 64 : (h + 1) * 64].rearrange("q j p -> q p j"),
            )

        out_v = out.rearrange("(m p) t -> p m t", p=P)

        def pieces_of(b):
            return [(0, 256), (256, 512)]

        def gather(b, between):
            parts = [keep.tile([P, HALF], F32, name=f"part{b}_{h}", tag=f"part{b}_{h}", align_bytes=64) for h in range(2)]
            for h in range(2):
                o = slice(h * HALF // 16, (h + 1) * HALF // 16)
                nc.vector.tensor_tensor(parts[h][:], xs[b][:].indirect(first[:, o]), pf_rows[h][:], MULT)
            pw = []
            for k, (lo, hi) in enumerate(pieces_of(b)):
                if k == 1 and between is not None:
                    between()
                piece = keep.tile(
                    [P, hi - lo], F32, name=f"pw{b}_{k}", align_bytes=64,
                    tag=f"part{b - 1}_0" if (b, k) == (TILES - 1, 0) else f"pw{b}_{k}",
                )
                h = lo // HALF
                nc.vector.tensor_tensor(
                    piece[:], xs[b][:].indirect(second[:, lo // 16 : hi // 16]), parts[h][:, lo - h * HALF : hi - h * HALF], MULT
                )
                pw.append(piece)
            return pw

        def turn(b, pw):
            pairs = keep.tile([P, 2, P, 2], BF16, name=f"pairs{b}", tag=f"pairs{b}", align_bytes=64)
            for piece, (lo, hi) in zip(pw, pieces_of(b)):
                cast = nc.vector.tensor_copy if (b, hi) == (TILES - 1, I) else nc.scalar.copy
                cast(pairs[:, :, lo // PACK : hi // PACK, :], piece[:].rearrange("t (p u e) -> t u p e", u=2, e=2))
            words = pairs[:].rearrange("t u p e -> t (u p e)").bitcast(F32)
            turned = psum.tile([P, 2, P], F32, name=f"turned{b}", tag="turn0" if b < 2 else f"acc{b - 2}_0")
            for u in range(2):
                nc.tensor.transpose(turned[:, u, :], words[:, u * P : (u + 1) * P], ident[:])
            grouped = keep.tile([P, P * PACK], BF16, name=f"grouped{b}", align_bytes=64)
            nc.scalar.copy(
                grouped[:].bitcast(F32).rearrange("p (t u) -> p t u", u=2), turned[:].rearrange("p u t -> p t u")
            )
            return grouped

        def quantise(b, grouped):
            codes = keep.tile([P, P], U32, name=f"codes{b}", tag="pf_row1" if b == TILES - 2 else f"part{b + 1}_0", align_bytes=64)
            scales = keep.tile([P, P], U8, name=f"scales{b}", align_bytes=64)
            nc.vector.quantize_mx(out=codes[:].bitcast(FP8X4), scales=scales[:], in_=grouped[:])
            return codes, scales

        def groups_of(b):
            return [(0,), (1,), (2,), (3,)] if b == TILES - 1 else [(0, 1, 2, 3)]

        def linear(b):
            tok = slice(b * P, (b + 1) * P)
            banks = [
                psum.tile([P, len(ms), P], F32, name=f"acc{b}_{g}", tag=f"acc{b}_{g}") for g, ms in enumerate(groups_of(b))
            ]
            for bank, ms in zip(banks, groups_of(b)):
                for k, m in enumerate(ms):
                    nc.tensor.matmul_mx(
                        out=bank[:, k, :],
                        lhsT=wc_sb[:, 2 * P * m : 2 * P * (m + 1)].bitcast(FP4X4),
                        lhsT_scale=wc_plane[:, P * m : P * (m + 1)],
                        rhs=cx_sb[b // 2][:, (b % 2) * P : (b % 2 + 1) * P].bitcast(FP8X4),
                        rhs_scale=cx_plane[:, tok],
                        start=(k == 0),
                        stop=False,
                    )
            return banks

        def multiply(b, banks, codes, scales):
            tok = slice(b * P, (b + 1) * P)
            last = b == TILES - 1
            for g, (bank, ms) in enumerate(zip(banks, groups_of(b))):
                for k, m in enumerate(ms):
                    nc.tensor.matmul_mx(
                        out=bank[:, k, :],
                        lhsT=w_sb[:, 2 * P * m : 2 * P * (m + 1)].bitcast(FP4X4),
                        lhsT_scale=w_plane[:, P * m : P * (m + 1)],
                        rhs=codes[:].bitcast(FP8X4),
                        rhs_scale=scales[:],
                        start=False,
                        stop=(k == len(ms) - 1),
                    )
                res = keep.tile([P, len(ms), P], F32, name=f"res{b}_{g}")
                if (last and g % 2 == 1) or b == TILES - 2:
                    nc.vector.tensor_copy(res[:], bank[:])
                else:
                    nc.scalar.copy(res[:], bank[:])
                nc.sync.dma_start(out_v[:, ms[0] : ms[-1] + 1, tok], res[:])

        pws = {}
        grouped = {}
        made = {}

        def quantise_before_last():
            made[TILES - 2] = quantise(TILES - 2, grouped[TILES - 2])

        sums = {}
        for step in range(TILES):
            last = step == TILES - 1
            if step >= 2:
                multiply(step - 2, sums[step - 2], *made[step - 2])
            pws[step] = gather(step, quantise_before_last if last else None)
            if last:
                multiply(step - 1, sums[step - 1], *made[step - 1])
            grouped[step] = turn(step, pws[step])
            if step < 2:
                for b in (2 * step, 2 * step + 1):
                    sums[b] = linear(b)
            if step >= 1 and not last:
                made[step - 1] = quantise(step - 1, grouped[step - 1])
        multiply(TILES - 1, sums[TILES - 1], *quantise(TILES - 1, grouped[TILES - 1]))
